import numpy as np
import ml_dtypes


def mxq(x, axis, fmt="e4m3"):
    dtype, down = {"e4m3": (ml_dtypes.float8_e4m3fn, 7), "e5m2": (ml_dtypes.float8_e5m2, 14)}[fmt]
    v = np.moveaxis(np.asarray(x, np.float32).astype(ml_dtypes.bfloat16).astype(np.float64), axis, -1)
    blocks = v.reshape(v.shape[:-1] + (-1, 32))
    amax = np.abs(blocks).max(-1, keepdims=True)
    byte = np.maximum(np.where(amax > 0, np.frexp(amax)[1] - 1 + 127, 0) - down, 1)
    scale = np.exp2(byte - 127.0)
    codes = (blocks / scale).astype(np.float32).astype(dtype).astype(np.float64)
    return np.moveaxis((codes * scale).reshape(v.shape), -1, axis)


WIDE = False


def mx_kscale(k):
    if not WIDE:
        return np.ones(k)
    levels = np.array([10, -10, 5, -5, 0])
    if k % 512:
        return np.exp2(np.random.permutation(np.resize(levels, k // 32))).repeat(32)
    a = np.empty((k // 512, 16))
    for p in range(k // 512):
        a[p, :8] = np.random.permutation(np.resize(levels, 8))
        for g in range(8):
            far = levels[np.abs(levels - a[p, g]) >= 10]
            a[p, g + 8] = far[np.random.randint(len(far))]
    return np.exp2(a.ravel()).repeat(32)


def f64(x):
    return np.asarray(x).astype(np.float64)


def striped(idx):
    return np.tile(idx.reshape(-1, 16).T, (8, 1)).astype(np.uint16)


def unstriped(offs):
    return offs[:16].T.reshape(-1).astype(np.int64)


def striped8(idx):
    return np.concatenate([x.reshape(-1, 16).T for x in idx]).astype(np.uint16)


def runs(offs, k):
    lists = np.stack([offs[16 * r : 16 * r + 16].T.reshape(-1) for r in range(8)]).astype(np.int64)
    return lists[np.arange(k) % 512 // 64]


def pack_weight(w):
    k, n = w.shape
    w = f64(np.asarray(w, np.float32).astype(ml_dtypes.bfloat16)).reshape(k // 32, 32, n)
    amax = np.abs(w).max(1)
    byte = np.clip(np.where(amax > 0, np.frexp(amax)[1] - 1 + 127 - 7, 1), 1, 254)
    scaled = (w * np.exp2(127.0 - byte)[:, None, :]).reshape(k, n).astype(np.float32)
    words = np.ascontiguousarray(scaled.reshape(k // 512, 128, 4, n).transpose(0, 1, 3, 2)).astype(ml_dtypes.float8_e4m3fn).view(np.uint8)
    return words, np.ascontiguousarray(byte.astype(np.uint8).reshape(k // 512, 16, n))


def unpack_weight(words, scales):
    g, p, n, _ = words.shape
    vals = np.ascontiguousarray(words).view(ml_dtypes.float8_e4m3fn).astype(np.float64) * np.repeat(np.exp2(scales.astype(np.float64) - 127.0), 8, axis=1)[..., None]
    return vals.transpose(0, 1, 3, 2).reshape(g * 512, n)


def relu(v):
    return np.maximum(v, 0.0)


def sigmoid(v):
    return 1.0 / (1.0 + np.exp(-np.maximum(v, -700.0)))


K, T, S, H, C = 512, 2048, 512, 512, 512


def setup_inputs():
    n = np.random.standard_normal
    s = mx_kscale(K)[:, None]
    packed_xT = pack_weight(n((K, T)) * s)
    return {
        "x_words": packed_xT[0],
        "x_scales": packed_xT[1],
        "w1": (n((K, H)) / np.sqrt(K) / s).astype(np.float32),
        "gs": (np.random.uniform(0.5, 1.5, (K, 1)) / s).astype(np.float32),
        "offs": striped(np.random.permutation(T)[:S]),
        "cand": striped(np.random.permutation(T)[:C]),
        "n1": striped8(np.stack([np.random.permutation(S) for _ in range(8)])),
        "n2": striped8(np.stack([np.random.permutation(S) for _ in range(8)])),
    }


def reference(x_words, x_scales, w1, gs, offs, cand, n1, n2):
    x_cand = unpack_weight(x_words, x_scales)[:, unstriped(cand)]
    xq = unpack_weight(x_words, x_scales)[:, unstriped(offs)]
    h = relu(mxq(f64(w1), 0, "e4m3").T @ xq)
    z = f64(gs) * h
    s = 0.0625 * ((x_cand.T @ mxq(z, 0, "e4m3")))
    mx = np.maximum(s[np.arange(C)[:, None], runs(n1, C)], s[np.arange(C)[:, None], runs(n2, C)])
    return relu(s - mx) * sigmoid(mx)

@@ -1,0 +1,163 @@
+from contextlib import ExitStack
+
+import concourse.mybir as mybir
+from concourse.masks import make_identity
+
+K, T, S, H, C = 512, 2048, 512, 512, 512
+FLOPS = 2 * K * H * S + 2 * H * C * S
+
+F32 = mybir.dt.float32
+BF16 = mybir.dt.bfloat16
+I32 = mybir.dt.int32
+U32 = mybir.dt.uint32
+U16 = mybir.dt.uint16
+U8 = mybir.dt.uint8
+FP8X4 = mybir.dt.float8_e4m3fn_x4
+ALU = mybir.AluOpType
+ACT = mybir.ActivationFunctionType
+
+P = 128
+PACK = 4
+HALF = 256
+
+
+def tile_picked_candwin_none_p_kernel(tc, x_words, x_scales, w1, gs, offs, cand, n1, n2, out):
+    nc = tc.nc
+    with ExitStack() as ctx:
+        keep = ctx.enter_context(tc.tile_pool(name="keep", bufs=1))
+        work = ctx.enter_context(tc.tile_pool(name="work", bufs=3))
+        psum = ctx.enter_context(tc.psum_pool(name="psum", bufs=8))
+
+        offs_t = keep.tile([P, S // 16], U16, name="offs_t")
+        cand_t = keep.tile([P, C // 16], U16, name="cand_t")
+        n1_t = keep.tile([P, S // 16], U16, name="n1_t")
+        n2_t = keep.tile([P, S // 16], U16, name="n2_t")
+        table_words = keep.tile([P, T], I32, name="table_words", align_bytes=64)
+        table_scales = keep.tile([P, T], U8, name="table_scales", align_bytes=64)
+        gs_t = keep.tile([P, 1, PACK], F32, name="gs_t")
+        w_raw = [keep.tile([P, PACK, P], F32, name="w_raw%d" % q) for q in range(4)]
+        w_view = w1.rearrange("(p j) c -> p j c", j=PACK)
+
+        nc.gpsimd.memset(table_scales[:].bitcast(I32), 0)
+        nc.sync.dma_start(offs_t[:], offs)
+        nc.sync.dma_start(w_raw[0][:], w_view[:, :, 0:P])
+        scale_rows = x_scales[0].bitcast(I32)
+        for q in range(4):
+            nc.sync.dma_start(table_scales[32 * q : 32 * q + 4, :].bitcast(I32), scale_rows[4 * q : 4 * q + 4, :])
+        nc.sync.dma_start(cand_t[:], cand)
+        nc.sync.dma_start(table_words[:], x_words[0].rearrange("p n t -> p (n t)").bitcast(I32))
+        for q in range(1, 4):
+            nc.sync.dma_start(w_raw[q][:], w_view[:, :, q * P : (q + 1) * P])
+        nc.sync.dma_start(gs_t[:], gs.rearrange("(p t) o -> p o t", t=PACK))
+        nc.sync.dma_start(n1_t[:], n1)
+        nc.sync.dma_start(n2_t[:], n2)
+
+        ident = keep.tile([P, P], F32, name="ident")
+        make_identity(nc, ident[:])
+
+        x_sc = keep.tile([P, S], U8, name="x_sc", align_bytes=64)
+        c_sc_raw = keep.tile([P, C], U8, name="c_sc_raw", align_bytes=64)
+        c_sc = keep.tile([P, C], U8, name="c_sc", align_bytes=64)
+        x_wd = [keep.tile([P, HALF], U32, name="x_wd%d" % h, align_bytes=64) for h in range(2)]
+        c_wd = keep.tile([P, C], U32, name="c_wd", align_bytes=64)
+        words_window = table_words[:].bitcast(U32)
+
+        nc.vector.tensor_copy(c_sc_raw[:], table_scales[:].indirect(cand_t[:]))
+        nc.vector.tensor_copy(x_sc[:], table_scales[:].indirect(offs_t[:]))
+        nc.vector.tensor_copy(c_sc[:].rearrange("k (t p) -> k t p", t=PACK), c_sc_raw[:].rearrange("k (p t) -> k t p", t=PACK))
+        for h in range(2):
+            nc.vector.tensor_copy(x_wd[h][:], words_window.indirect(offs_t[:, 16 * h : 16 * h + 16]))
+        nc.vector.tensor_copy(c_wd[:].rearrange("k (t p) -> k p t", t=PACK), words_window.indirect(cand_t[:]))
+
+        w_bf = keep.tile([P, PACK * H], BF16, name="w_bf", align_bytes=64)
+        w_bf_view = w_bf[:].rearrange("p (t m j) -> p m j t", t=PACK, j=PACK)
+        for q in range(4):
+            nc.scalar.copy(w_bf_view[:, 32 * q : 32 * q + 32, :, :], w_raw[q][:].rearrange("p j (m t) -> p m j t", t=PACK))
+        w_wd = keep.tile([P, H], U32, name="w_wd", align_bytes=64)
+        w_sc = keep.tile([P, H], U8, name="w_sc", align_bytes=64)
+        nc.vector.quantize_mx(out=w_wd[:].bitcast(FP8X4), scales=w_sc[:], in_=w_bf[:])
+
+        h_banks = []
+        for c in range(4):
+            bank = psum.tile([P, PACK, P], F32, name="h_bank%d" % c, tag="bank")
+            cols = slice((c % 2) * P, (c % 2 + 1) * P)
+            for t in range(PACK):
+                ch = slice(t * P, (t + 1) * P)
+                nc.tensor.matmul_mx(out=bank[:, t, :], lhsT=w_wd[:, ch].bitcast(FP8X4), lhsT_scale=w_sc[:, ch],
+                                    rhs=x_wd[c // 2][:, cols].bitcast(FP8X4), rhs_scale=x_sc[:, c * P : (c + 1) * P],
+                                    start=True, stop=True)
+            h_banks.append(bank)
+        s_banks = [psum.tile([P, S], F32, name="s_bank%d" % t, tag="bank") for t in range(PACK)]
+        s_sb = [keep.tile([P, S], F32, name="s_sb%d" % t) for t in range(PACK)]
+        z_bf = [keep.tile([P, P, PACK], BF16, name="z_bf%d" % c, align_bytes=64) for c in range(4)]
+        z_wd = [keep.tile([P, P], U32, name="z_wd%d" % c, align_bytes=64) for c in range(4)]
+        z_sc = [keep.tile([P, P], U8, name="z_sc%d" % c, align_bytes=64) for c in range(4)]
+
+        def make_z(c):
+            nc.vector.scalar_tensor_tensor(out=z_bf[c][:], in0=h_banks[c][:].rearrange("p t n -> p n t"), scalar=0.0,
+                                           in1=gs_t[:].to_broadcast([P, P, PACK]), op0=ALU.max, op1=ALU.mult)
+
+        def score(c):
+            nc.vector.quantize_mx(out=z_wd[c][:].bitcast(FP8X4), scales=z_sc[c][:], in_=z_bf[c][:].rearrange("p n t -> p (n t)"))
+            cols = slice(c * P, (c + 1) * P)
+            for t in range(PACK):
+                rows = slice(t * P, (t + 1) * P)
+                nc.tensor.matmul_mx(out=s_banks[t][:, cols], lhsT=c_wd[:, rows].bitcast(FP8X4), lhsT_scale=c_sc[:, rows],
+                                    rhs=z_wd[c][:].bitcast(FP8X4), rhs_scale=z_sc[c][:], start=True, stop=True)
+            if c >= 2:
+                done = slice(0, 3 * P) if c == 2 else cols
+                nc.scalar.activation(s_sb[0][:, done], s_banks[0][:, done], ACT.Copy, scale=0.0625)
+
+        make_z(0)
+        for c in range(1, 4):
+            make_z(c)
+            score(c - 1)
+        score(3)
+        for t in range(1, PACK):
+            nc.scalar.activation(s_sb[t][:], s_banks[t][:], ACT.Copy, scale=0.0625)
+
+        out_view = out.rearrange("(p t) j -> p t j", t=PACK)
+        halves = [slice(h * HALF, (h + 1) * HALF) for h in range(2)]
+        state = {}
+
+        def fetch(t):
+            pair = work.tile([P, 2, S], F32, name="pair", bufs=2)
+            for h in range(2):
+                for which, lst in enumerate((n1_t, n2_t)):
+                    nc.vector.tensor_scalar(pair[:, which, halves[h]], s_sb[t][:].indirect(lst[:, 16 * h : 16 * h + 16]), -1.0, 0.0, ALU.mult, ALU.add)
+            nmx = work.tile([P, S], F32, name="nmx", bufs=4)
+            for h in range(2):
+                nc.vector.tensor_tensor(nmx[:, halves[h]], pair[:, 0, halves[h]], pair[:, 1, halves[h]], ALU.min)
+            sig = work.tile([P, S], F32, name="sig", bufs=4)
+            if t == PACK - 1:
+                d = work.tile([P, S], F32, name="d", bufs=1)
+                for h in range(2):
+                    nc.scalar.activation(sig[:, halves[h]], nmx[:, halves[h]], ACT.Sigmoid, scale=-1.0)
+                    nc.vector.tensor_tensor(d[:, halves[h]], s_sb[t][:, halves[h]], nmx[:, halves[h]], ALU.add)
+                state[t] = (d, sig)
+                return
+            turned = psum.tile([P, S], F32, name="turned", tag="bank")
+            for b in range(4):
+                blk = slice(b * P, (b + 1) * P)
+                nc.tensor.matmul(turned[:, blk], s_sb[t][:, blk], ident[:], start=True, stop=False, is_transpose=True)
+                nc.tensor.matmul(turned[:, blk], nmx[:, blk], ident[:], start=False, stop=True, is_transpose=True)
+            nc.scalar.activation(sig[:], nmx[:], ACT.Sigmoid, scale=-1.0)
+            nc.scalar.copy(pair[:, 0, :], turned[:])
+            d = psum.tile([P, S], F32, name="d_bank", tag="bank")
+            for b in range(4):
+                blk = slice(b * P, (b + 1) * P)
+                nc.tensor.transpose(d[:, blk], pair[:, 0, blk], ident[:])
+            state[t] = (d, sig)
+
+        def finish(t):
+            d, sig = state[t]
+            res = work.tile([P, S], F32, name="res", bufs=4)
+            for cols in (halves if t == PACK - 1 else [slice(0, S)]):
+                nc.vector.scalar_tensor_tensor(out=res[:, cols], in0=d[:, cols], scalar=0.0, in1=sig[:, cols], op0=ALU.max, op1=ALU.mult)
+                nc.sync.dma_start(out_view[:, t, cols], res[:, cols])
+
+        for step in range(PACK + 2):
+            if step >= 2:
+                finish(step - 2)
+            if step < PACK:
+                fetch(step)

@@ -25,8 +25,9 @@ def tile_picked_candwin_none_p_kernel(tc, x_words, x_scales, w1, gs, offs, cand,
     nc = tc.nc
     with ExitStack() as ctx:
         keep = ctx.enter_context(tc.tile_pool(name="keep", bufs=1))
-        work = ctx.enter_context(tc.tile_pool(name="work", bufs=3))
-        psum = ctx.enter_context(tc.psum_pool(name="psum", bufs=8))
+        work = ctx.enter_context(tc.tile_pool(name="work", bufs=2))
+        psum = ctx.enter_context(tc.psum_pool(name="psum", bufs=1))
+        banks = [psum.tile([P, S], F32, name="bank%d" % i) for i in range(8)]
 
         offs_t = keep.tile([P, S // 16], U16, name="offs_t")
         cand_t = keep.tile([P, C // 16], U16, name="cand_t")
@@ -35,19 +36,21 @@ def tile_picked_candwin_none_p_kernel(tc, x_words, x_scales, w1, gs, offs, cand,
         table_words = keep.tile([P, T], I32, name="table_words", align_bytes=64)
         table_scales = keep.tile([P, T], U8, name="table_scales", align_bytes=64)
         gs_t = keep.tile([P, 1, PACK], F32, name="gs_t")
-        w_raw = [keep.tile([P, PACK, P], F32, name="w_raw%d" % q) for q in range(4)]
+        windows = [keep.tile([P, 2 * S], F32, name="window%d" % q) for q in range(4)]
+        w_raw = [win[:, S : 2 * S].rearrange("p (j c) -> p j c", j=PACK) for win in windows]
+        s_sb = [win[:, 0:S] for win in windows]
         w_view = w1.rearrange("(p j) c -> p j c", j=PACK)
 
         nc.gpsimd.memset(table_scales[:].bitcast(I32), 0)
         nc.sync.dma_start(offs_t[:], offs)
-        nc.sync.dma_start(w_raw[0][:], w_view[:, :, 0:P])
+        nc.sync.dma_start(w_raw[0], w_view[:, :, 0:P])
         scale_rows = x_scales[0].bitcast(I32)
         for q in range(4):
             nc.sync.dma_start(table_scales[32 * q : 32 * q + 4, :].bitcast(I32), scale_rows[4 * q : 4 * q + 4, :])
         nc.sync.dma_start(cand_t[:], cand)
         nc.sync.dma_start(table_words[:], x_words[0].rearrange("p n t -> p (n t)").bitcast(I32))
         for q in range(1, 4):
-            nc.sync.dma_start(w_raw[q][:], w_view[:, :, q * P : (q + 1) * P])
+            nc.sync.dma_start(w_raw[q], w_view[:, :, q * P : (q + 1) * P])
         nc.sync.dma_start(gs_t[:], gs.rearrange("(p t) o -> p o t", t=PACK))
         nc.sync.dma_start(n1_t[:], n1)
         nc.sync.dma_start(n2_t[:], n2)
@@ -57,104 +60,99 @@ def tile_picked_candwin_none_p_kernel(tc, x_words, x_scales, w1, gs, offs, cand,
 
         x_sc = keep.tile([P, S], U8, name="x_sc", align_bytes=64)
         c_sc_raw = keep.tile([P, C], U8, name="c_sc_raw", align_bytes=64)
-        c_sc = keep.tile([P, C], U8, name="c_sc", align_bytes=64)
-        x_wd = [keep.tile([P, HALF], U32, name="x_wd%d" % h, align_bytes=64) for h in range(2)]
+        x_wd = keep.tile([P, S], U32, name="x_wd", align_bytes=64)
         c_wd = keep.tile([P, C], U32, name="c_wd", align_bytes=64)
         words_window = table_words[:].bitcast(U32)
 
         nc.vector.tensor_copy(c_sc_raw[:], table_scales[:].indirect(cand_t[:]))
         nc.vector.tensor_copy(x_sc[:], table_scales[:].indirect(offs_t[:]))
-        nc.vector.tensor_copy(c_sc[:].rearrange("k (t p) -> k t p", t=PACK), c_sc_raw[:].rearrange("k (p t) -> k t p", t=PACK))
-        for h in range(2):
-            nc.vector.tensor_copy(x_wd[h][:], words_window.indirect(offs_t[:, 16 * h : 16 * h + 16]))
+        nc.vector.tensor_copy(x_wd[:], words_window.indirect(offs_t[:]))
         nc.vector.tensor_copy(c_wd[:].rearrange("k (t p) -> k p t", t=PACK), words_window.indirect(cand_t[:]))
 
-        w_bf = keep.tile([P, PACK * H], BF16, name="w_bf", align_bytes=64)
+        w_bf = keep.tile([P, PACK * H], BF16, name="w_bf", tag="stage", align_bytes=64)
         w_bf_view = w_bf[:].rearrange("p (t m j) -> p m j t", t=PACK, j=PACK)
         for q in range(4):
-            nc.scalar.copy(w_bf_view[:, 32 * q : 32 * q + 32, :, :], w_raw[q][:].rearrange("p j (m t) -> p m j t", t=PACK))
-        w_wd = keep.tile([P, H], U32, name="w_wd", align_bytes=64)
-        w_sc = keep.tile([P, H], U8, name="w_sc", align_bytes=64)
-        nc.vector.quantize_mx(out=w_wd[:].bitcast(FP8X4), scales=w_sc[:], in_=w_bf[:])
+            nc.scalar.copy(w_bf_view[:, 32 * q : 32 * q + 32, :, :], w_raw[q].rearrange("p j (m t) -> p m j t", t=PACK))
+        w_wd = [keep.tile([P, P], U32, name="w_wd%d" % t, align_bytes=64) for t in range(PACK)]
+        w_sc = [keep.tile([P, P], U8, name="w_sc%d" % t, align_bytes=64) for t in range(PACK)]
+        for t in range(PACK):
+            nc.vector.quantize_mx(out=w_wd[t][:].bitcast(FP8X4), scales=w_sc[t][:], in_=w_bf[:, t * H : (t + 1) * H])
+        c_sc = keep.tile([P, C], U8, name="c_sc", tag="stage", align_bytes=64)
+        nc.vector.tensor_copy(c_sc[:].rearrange("k (t p) -> k t p", t=PACK), c_sc_raw[:].rearrange("k (p t) -> k t p", t=PACK))
 
         h_banks = []
         for c in range(4):
-            bank = psum.tile([P, PACK, P], F32, name="h_bank%d" % c, tag="bank")
-            cols = slice((c % 2) * P, (c % 2 + 1) * P)
-            for t in range(PACK):
-                ch = slice(t * P, (t + 1) * P)
-                nc.tensor.matmul_mx(out=bank[:, t, :], lhsT=w_wd[:, ch].bitcast(FP8X4), lhsT_scale=w_sc[:, ch],
-                                    rhs=x_wd[c // 2][:, cols].bitcast(FP8X4), rhs_scale=x_sc[:, c * P : (c + 1) * P],
-                                    start=True, stop=True)
-            h_banks.append(bank)
-        s_banks = [psum.tile([P, S], F32, name="s_bank%d" % t, tag="bank") for t in range(PACK)]
-        s_sb = [keep.tile([P, S], F32, name="s_sb%d" % t) for t in range(PACK)]
-        z_bf = [keep.tile([P, P, PACK], BF16, name="z_bf%d" % c, align_bytes=64) for c in range(4)]
-        z_wd = [keep.tile([P, P], U32, name="z_wd%d" % c, align_bytes=64) for c in range(4)]
-        z_sc = [keep.tile([P, P], U8, name="z_sc%d" % c, align_bytes=64) for c in range(4)]
-
-        def make_z(c):
-            nc.vector.scalar_tensor_tensor(out=z_bf[c][:], in0=h_banks[c][:].rearrange("p t n -> p n t"), scalar=0.0,
-                                           in1=gs_t[:].to_broadcast([P, P, PACK]), op0=ALU.max, op1=ALU.mult)
-
-        def score(c):
-            nc.vector.quantize_mx(out=z_wd[c][:].bitcast(FP8X4), scales=z_sc[c][:], in_=z_bf[c][:].rearrange("p n t -> p (n t)"))
+            bank = banks[c][:].rearrange("p (t n) -> p t n", t=PACK)
             cols = slice(c * P, (c + 1) * P)
             for t in range(PACK):
-                rows = slice(t * P, (t + 1) * P)
-                nc.tensor.matmul_mx(out=s_banks[t][:, cols], lhsT=c_wd[:, rows].bitcast(FP8X4), lhsT_scale=c_sc[:, rows],
-                                    rhs=z_wd[c][:].bitcast(FP8X4), rhs_scale=z_sc[c][:], start=True, stop=True)
-            if c >= 2:
-                done = slice(0, 3 * P) if c == 2 else cols
-                nc.scalar.activation(s_sb[0][:, done], s_banks[0][:, done], ACT.Copy, scale=0.0625)
+                nc.tensor.matmul_mx(out=bank[:, t, :], lhsT=w_wd[t][:].bitcast(FP8X4), lhsT_scale=w_sc[t][:],
+                                    rhs=x_wd[:, cols].bitcast(FP8X4), rhs_scale=x_sc[:, cols],
+                                    start=True, stop=True)
+            h_banks.append(bank)
+        z_bf = [keep.tile([P, P, PACK], BF16, name="z_bf%d" % c, align_bytes=64) for c in range(4)]
+        z_wd = keep.tile([P, S], U32, name="z_wd", align_bytes=64)
+        z_sc = keep.tile([P, S], U8, name="z_sc", align_bytes=64)
+        first_banks = banks[4:6]
+
+        def make_z(c):
+            nc.vector.scalar_tensor_tensor(out=z_bf[c][:], in0=h_banks[c].rearrange("p t n -> p n t"), scalar=0.0,
+                                           in1=gs_t[:].to_broadcast([P, P, PACK]), op0=ALU.max, op1=ALU.mult)
+
+        def score(t, cols, bank):
+            rows = slice(t * P, (t + 1) * P)
+            nc.tensor.matmul_mx(out=bank, lhsT=c_wd[:, rows].bitcast(FP8X4), lhsT_scale=c_sc[:, rows],
+                                rhs=z_wd[:, cols].bitcast(FP8X4), rhs_scale=z_sc[:, cols], start=True, stop=True)
+            nc.scalar.activation(s_sb[t][:, cols], bank, ACT.Copy, scale=0.0625)
+
+        def quantise_z(c):
+            cols = slice(c * P, (c + 1) * P)
+            nc.vector.quantize_mx(out=z_wd[:, cols].bitcast(FP8X4), scales=z_sc[:, cols], in_=z_bf[c][:].rearrange("p n t -> p (n t)"))
+            score(0, cols, first_banks[c % 2][:, (c // 2) * P : (c // 2 + 1) * P])
 
         make_z(0)
         for c in range(1, 4):
             make_z(c)
-            score(c - 1)
-        score(3)
+            quantise_z(c - 1)
+        quantise_z(3)
         for t in range(1, PACK):
-            nc.scalar.activation(s_sb[t][:], s_banks[t][:], ACT.Copy, scale=0.0625)
+            score(t, slice(0, S), banks[(6, 7, 0)[t - 1]][:])
 
         out_view = out.rearrange("(p t) j -> p t j", t=PACK)
         halves = [slice(h * HALF, (h + 1) * HALF) for h in range(2)]
-        state = {}
+        blocks = [slice(b * P, (b + 1) * P) for b in range(4)]
+        nmx = [keep.tile([P, S], F32, name="nmx%d" % i) for i in range(2)]
+        d_last = keep.tile([P, S], F32, name="d_last")
+        sig = [keep.tile([P, S], F32, name="sig%d" % t) for t in range(PACK)]
+        res = [keep.tile([P, S], F32, name="res%d" % t) for t in range(PACK)]
+        d_of = [banks[2], banks[3], banks[2], d_last]
+        turned = banks[5]
 
         def fetch(t):
-            pair = work.tile([P, 2, S], F32, name="pair", bufs=2)
+            win = windows[t][:]
+            pair = work.tile([P, 2, S], F32, name="pair")
+            a, b, m = pair[:, 0, :], pair[:, 1, :], nmx[t % 2]
+            nc.vector.tensor_scalar(b, win.indirect(n2_t[:]), -1.0, 0.0, ALU.mult, ALU.add)
             for h in range(2):
-                for which, lst in enumerate((n1_t, n2_t)):
-                    nc.vector.tensor_scalar(pair[:, which, halves[h]], s_sb[t][:].indirect(lst[:, 16 * h : 16 * h + 16]), -1.0, 0.0, ALU.mult, ALU.add)
-            nmx = work.tile([P, S], F32, name="nmx", bufs=4)
-            for h in range(2):
-                nc.vector.tensor_tensor(nmx[:, halves[h]], pair[:, 0, halves[h]], pair[:, 1, halves[h]], ALU.min)
-            sig = work.tile([P, S], F32, name="sig", bufs=4)
+                nc.vector.tensor_scalar(a[:, halves[h]], win.indirect(n1_t[:, 16 * h : 16 * h + 16]), -1.0, 0.0, ALU.mult, ALU.add)
+            for cols in halves:
+                nc.vector.tensor_tensor(m[:, cols], a[:, cols], b[:, cols], ALU.min)
             if t == PACK - 1:
-                d = work.tile([P, S], F32, name="d", bufs=1)
-                for h in range(2):
-                    nc.scalar.activation(sig[:, halves[h]], nmx[:, halves[h]], ACT.Sigmoid, scale=-1.0)
-                    nc.vector.tensor_tensor(d[:, halves[h]], s_sb[t][:, halves[h]], nmx[:, halves[h]], ALU.add)
-                state[t] = (d, sig)
+                for cols in halves:
+                    nc.scalar.activation(sig[t][:, cols], m[:, cols], ACT.Sigmoid, scale=-1.0)
+                    nc.vector.tensor_tensor(d_last[:, cols], s_sb[t][:, cols], m[:, cols], ALU.add)
                 return
-            turned = psum.tile([P, S], F32, name="turned", tag="bank")
-            for b in range(4):
-                blk = slice(b * P, (b + 1) * P)
-                nc.tensor.matmul(turned[:, blk], s_sb[t][:, blk], ident[:], start=True, stop=False, is_transpose=True)
-                nc.tensor.matmul(turned[:, blk], nmx[:, blk], ident[:], start=False, stop=True, is_transpose=True)
-            nc.scalar.activation(sig[:], nmx[:], ACT.Sigmoid, scale=-1.0)
-            nc.scalar.copy(pair[:, 0, :], turned[:])
-            d = psum.tile([P, S], F32, name="d_bank", tag="bank")
-            for b in range(4):
-                blk = slice(b * P, (b + 1) * P)
-                nc.tensor.transpose(d[:, blk], pair[:, 0, blk], ident[:])
-            state[t] = (d, sig)
+            nc.scalar.activation(sig[t][:], m[:], ACT.Sigmoid, scale=-1.0)
+            for i, term in enumerate((s_sb[t], m)):
+                for n, blk in enumerate(blocks):
+                    nc.tensor.matmul(turned[:, blk], term[:, blk], ident[:], start=(i == 0 and n == 0), stop=(i == 1 and n == 3), is_transpose=True)
+            nc.scalar.copy(b, turned[:])
+            for blk in blocks:
+                nc.tensor.transpose(d_of[t][:, blk], b[:, blk], ident[:])
 
         def finish(t):
-            d, sig = state[t]
-            res = work.tile([P, S], F32, name="res", bufs=4)
             for cols in (halves if t == PACK - 1 else [slice(0, S)]):
-                nc.vector.scalar_tensor_tensor(out=res[:, cols], in0=d[:, cols], scalar=0.0, in1=sig[:, cols], op0=ALU.max, op1=ALU.mult)
-                nc.sync.dma_start(out_view[:, t, cols], res[:, cols])
+                nc.vector.scalar_tensor_tensor(out=res[t][:, cols], in0=d_of[t][:, cols], scalar=0.0, in1=sig[t][:, cols], op0=ALU.max, op1=ALU.mult)
+                nc.sync.dma_start(out_view[:, t, cols], res[t][:, cols])
 
         for step in range(PACK + 2):
             if step >= 2:

from contextlib import ExitStack

import concourse.mybir as mybir
from concourse.masks import make_identity

K, T, S, H, C = 512, 2048, 512, 512, 512
FLOPS = 2 * K * H * S + 2 * H * C * S

F32 = mybir.dt.float32
BF16 = mybir.dt.bfloat16
I32 = mybir.dt.int32
U32 = mybir.dt.uint32
U16 = mybir.dt.uint16
U8 = mybir.dt.uint8
FP8X4 = mybir.dt.float8_e4m3fn_x4
ALU = mybir.AluOpType
ACT = mybir.ActivationFunctionType

P = 128
PACK = 4
HALF = 256


def tile_picked_candwin_none_p_kernel(tc, x_words, x_scales, w1, gs, offs, cand, n1, n2, out):
    nc = tc.nc
    with ExitStack() as ctx:
        keep = ctx.enter_context(tc.tile_pool(name="keep", bufs=1))
        work = ctx.enter_context(tc.tile_pool(name="work", bufs=2))
        psum = ctx.enter_context(tc.psum_pool(name="psum", bufs=1))
        banks = [psum.tile([P, S], F32, name="bank%d" % i) for i in range(8)]

        offs_t = keep.tile([P, S // 16], U16, name="offs_t")
        cand_t = keep.tile([P, C // 16], U16, name="cand_t")
        n1_t = keep.tile([P, S // 16], U16, name="n1_t")
        n2_t = keep.tile([P, S // 16], U16, name="n2_t")
        table_words = keep.tile([P, T], I32, name="table_words", align_bytes=64)
        table_scales = keep.tile([P, T], U8, name="table_scales", align_bytes=64)
        gs_t = keep.tile([P, 1, PACK], F32, name="gs_t")
        windows = [keep.tile([P, 2 * S], F32, name="window%d" % q) for q in range(4)]
        w_raw = [win[:, S : 2 * S].rearrange("p (j c) -> p j c", j=PACK) for win in windows]
        s_sb = [win[:, 0:S] for win in windows]
        w_view = w1.rearrange("(p j) c -> p j c", j=PACK)

        nc.gpsimd.memset(table_scales[:].bitcast(I32), 0)
        nc.sync.dma_start(offs_t[:], offs)
        nc.sync.dma_start(w_raw[0], w_view[:, :, 0:P])
        scale_rows = x_scales[0].bitcast(I32)
        for q in range(4):
            nc.sync.dma_start(table_scales[32 * q : 32 * q + 4, :].bitcast(I32), scale_rows[4 * q : 4 * q + 4, :])
        nc.sync.dma_start(cand_t[:], cand)
        nc.sync.dma_start(table_words[:], x_words[0].rearrange("p n t -> p (n t)").bitcast(I32))
        for q in range(1, 4):
            nc.sync.dma_start(w_raw[q], w_view[:, :, q * P : (q + 1) * P])
        nc.sync.dma_start(gs_t[:], gs.rearrange("(p t) o -> p o t", t=PACK))
        nc.sync.dma_start(n1_t[:], n1)
        nc.sync.dma_start(n2_t[:], n2)

        ident = keep.tile([P, P], F32, name="ident")
        make_identity(nc, ident[:])

        x_sc = keep.tile([P, S], U8, name="x_sc", align_bytes=64)
        c_sc_raw = keep.tile([P, C], U8, name="c_sc_raw", align_bytes=64)
        x_wd = keep.tile([P, S], U32, name="x_wd", align_bytes=64)
        c_wd = keep.tile([P, C], U32, name="c_wd", align_bytes=64)
        words_window = table_words[:].bitcast(U32)

        nc.vector.tensor_copy(c_sc_raw[:], table_scales[:].indirect(cand_t[:]))
        nc.vector.tensor_copy(x_sc[:], table_scales[:].indirect(offs_t[:]))
        nc.vector.tensor_copy(x_wd[:], words_window.indirect(offs_t[:]))
        nc.vector.tensor_copy(c_wd[:].rearrange("k (t p) -> k p t", t=PACK), words_window.indirect(cand_t[:]))

        w_bf = keep.tile([P, PACK * H], BF16, name="w_bf", tag="stage", align_bytes=64)
        w_bf_view = w_bf[:].rearrange("p (t m j) -> p m j t", t=PACK, j=PACK)
        for q in range(4):
            nc.scalar.copy(w_bf_view[:, 32 * q : 32 * q + 32, :, :], w_raw[q].rearrange("p j (m t) -> p m j t", t=PACK))
        w_wd = [keep.tile([P, P], U32, name="w_wd%d" % t, align_bytes=64) for t in range(PACK)]
        w_sc = [keep.tile([P, P], U8, name="w_sc%d" % t, align_bytes=64) for t in range(PACK)]
        for t in range(PACK):
            nc.vector.quantize_mx(out=w_wd[t][:].bitcast(FP8X4), scales=w_sc[t][:], in_=w_bf[:, t * H : (t + 1) * H])
        c_sc = keep.tile([P, C], U8, name="c_sc", tag="stage", align_bytes=64)
        nc.vector.tensor_copy(c_sc[:].rearrange("k (t p) -> k t p", t=PACK), c_sc_raw[:].rearrange("k (p t) -> k t p", t=PACK))

        h_banks = []
        for c in range(4):
            bank = banks[c][:].rearrange("p (t n) -> p t n", t=PACK)
            cols = slice(c * P, (c + 1) * P)
            for t in range(PACK):
                nc.tensor.matmul_mx(out=bank[:, t, :], lhsT=w_wd[t][:].bitcast(FP8X4), lhsT_scale=w_sc[t][:],
                                    rhs=x_wd[:, cols].bitcast(FP8X4), rhs_scale=x_sc[:, cols],
                                    start=True, stop=True)
            h_banks.append(bank)
        z_bf = [keep.tile([P, P, PACK], BF16, name="z_bf%d" % c, align_bytes=64) for c in range(4)]
        z_wd = keep.tile([P, S], U32, name="z_wd", align_bytes=64)
        z_sc = keep.tile([P, S], U8, name="z_sc", align_bytes=64)
        first_banks = banks[4:6]

        def make_z(c):
            nc.vector.scalar_tensor_tensor(out=z_bf[c][:], in0=h_banks[c].rearrange("p t n -> p n t"), scalar=0.0,
                                           in1=gs_t[:].to_broadcast([P, P, PACK]), op0=ALU.max, op1=ALU.mult)

        def score(t, cols, bank):
            rows = slice(t * P, (t + 1) * P)
            nc.tensor.matmul_mx(out=bank, lhsT=c_wd[:, rows].bitcast(FP8X4), lhsT_scale=c_sc[:, rows],
                                rhs=z_wd[:, cols].bitcast(FP8X4), rhs_scale=z_sc[:, cols], start=True, stop=True)
            nc.scalar.activation(s_sb[t][:, cols], bank, ACT.Copy, scale=0.0625)

        def quantise_z(c):
            cols = slice(c * P, (c + 1) * P)
            nc.vector.quantize_mx(out=z_wd[:, cols].bitcast(FP8X4), scales=z_sc[:, cols], in_=z_bf[c][:].rearrange("p n t -> p (n t)"))
            score(0, cols, first_banks[c % 2][:, (c // 2) * P : (c // 2 + 1) * P])

        make_z(0)
        for c in range(1, 4):
            make_z(c)
            quantise_z(c - 1)
        quantise_z(3)
        for t in range(1, PACK):
            score(t, slice(0, S), banks[(6, 7, 0)[t - 1]][:])

        out_view = out.rearrange("(p t) j -> p t j", t=PACK)
        halves = [slice(h * HALF, (h + 1) * HALF) for h in range(2)]
        blocks = [slice(b * P, (b + 1) * P) for b in range(4)]
        nmx = [keep.tile([P, S], F32, name="nmx%d" % i) for i in range(2)]
        d_last = keep.tile([P, S], F32, name="d_last")
        sig = [keep.tile([P, S], F32, name="sig%d" % t) for t in range(PACK)]
        res = [keep.tile([P, S], F32, name="res%d" % t) for t in range(PACK)]
        d_of = [banks[2], banks[3], banks[2], d_last]
        turned = banks[5]

        def fetch(t):
            win = windows[t][:]
            pair = work.tile([P, 2, S], F32, name="pair")
            a, b, m = pair[:, 0, :], pair[:, 1, :], nmx[t % 2]
            nc.vector.tensor_scalar(b, win.indirect(n2_t[:]), -1.0, 0.0, ALU.mult, ALU.add)
            for h in range(2):
                nc.vector.tensor_scalar(a[:, halves[h]], win.indirect(n1_t[:, 16 * h : 16 * h + 16]), -1.0, 0.0, ALU.mult, ALU.add)
            for cols in halves:
                nc.vector.tensor_tensor(m[:, cols], a[:, cols], b[:, cols], ALU.min)
            if t == PACK - 1:
                for cols in halves:
                    nc.scalar.activation(sig[t][:, cols], m[:, cols], ACT.Sigmoid, scale=-1.0)
                    nc.vector.tensor_tensor(d_last[:, cols], s_sb[t][:, cols], m[:, cols], ALU.add)
                return
            nc.scalar.activation(sig[t][:], m[:], ACT.Sigmoid, scale=-1.0)
            for i, term in enumerate((s_sb[t], m)):
                for n, blk in enumerate(blocks):
                    nc.tensor.matmul(turned[:, blk], term[:, blk], ident[:], start=(i == 0 and n == 0), stop=(i == 1 and n == 3), is_transpose=True)
            nc.scalar.copy(b, turned[:])
            for blk in blocks:
                nc.tensor.transpose(d_of[t][:, blk], b[:, blk], ident[:])

        def finish(t):
            for cols in (halves if t == PACK - 1 else [slice(0, S)]):
                nc.vector.scalar_tensor_tensor(out=res[t][:, cols], in0=d_of[t][:, cols], scalar=0.0, in1=sig[t][:, cols], op0=ALU.max, op1=ALU.mult)
                nc.sync.dma_start(out_view[:, t, cols], res[t][:, cols])

        for step in range(PACK + 2):
            if step >= 2:
                finish(step - 2)
            if step < PACK:
                fetch(step)
